import numpy as np
CORES = [15,47,79,175,207]
N = 5
F = 128
TK = N * F
EPS = 0.01
def setup_inputs(rng):
    return {"x": rng.standard_normal((N, 128, TK), dtype=np.float32) * (0.5 + np.abs(rng.standard_normal((1, 1, TK), dtype=np.float32)))}
def setup_inputs_big(rng):
    d = setup_inputs(rng)
    for k in ("x",): d[k] = (d[k].astype(np.float32) * 1024.0).astype(d[k].dtype)
    return d
def setup_inputs_small(rng):
    d = setup_inputs(rng)
    for k in ("x",): d[k] = (d[k].astype(np.float32) * (1 / 1024.0)).astype(d[k].dtype)
    return d
def setup_inputs_apart(rng):
    d = setup_inputs(rng)
    f = (10.0 ** rng.permutation(np.linspace(-1.5, 1.5, N))).astype(np.float32).reshape(N, 1, 1)
    for k in ("x",): d[k] = (d[k].astype(np.float32) * f).astype(d[k].dtype)
    return d
def setup_inputs_mixed(rng):
    d = setup_inputs(rng)
    f = (10.0 ** rng.uniform(-3, 3, (1, 1, TK))).astype(np.float32); shape = rng.integers(2, size=(1, 1, TK))
    for k in ("x",):
        x = d[k].astype(np.float32)
        other = x * np.where(rng.random((1, 128, TK)) < 0.5, 0.1, 1.0).astype(np.float32)
        d[k] = (np.where(shape == 1, other, x) * f).astype(d[k].dtype)
    return d
def reference(x):
    s = x.astype(np.float64).sum(axis=0)
    n = s / np.sqrt((s ** 2).sum(axis=0) / 128 + EPS)
    return {"y": np.stack([n[:, F * r:F * r + F] for r in range(N)]).astype(np.float32)}

@@ -1,0 +1,149 @@
+from concourse.mybir import AluOpType, AxisListType, ActivationFunctionType
+
+F = 128
+NR = 5
+EPS = 0.01
+N1, N2 = 67, 63
+RHO = 4.0 ** (1.0 / 64.0)
+KAP = 16.0 * RHO ** -0.25
+
+SCRATCH = {
+    "xs": ("sbuf", [128, NR * F], "float32"),
+    "land": ("sbuf", [128, (NR - 1) * F], "float32"),
+    "ones": ("sbuf", [128, F], "float32"),
+    "ident": ("sbuf", [128, F], "float32"),
+    "c128": ("sbuf", [128, 1], "float32"),
+    "epsc": ("sbuf", [128, 1], "float32"),
+    "rat": ("sbuf", [128, N1 + N2], "float32"),
+    "lad": ("sbuf", [128, N1 + N2], "float32"),
+    "fac": ("sbuf", [128, N1 + N2], "float32"),
+    "p1": ("sbuf", [128, 1], "float32"),
+    "p2": ("sbuf", [128, 1], "float32"),
+    "w": ("sbuf", [128, 1], "float32"),
+    "t": ("sbuf", [128, 1], "float32"),
+    "b": ("sbuf", [128, 1], "float32"),
+    "c": ("sbuf", [128, 1], "float32"),
+    "s": ("sbuf", [128, F], "float32"),
+    "sq": ("sbuf", [128, F], "float32"),
+    "d1": ("sbuf", [128, F], "float32"),
+    "dg": ("sbuf", [128, F], "float32"),
+    "yv": ("sbuf", [128, F], "float32"),
+    "acc": ("psum", [128, 512], "float32"),
+    "vps": ("psum", [128, 512], "float32"),
+    "rb": ("psum", [128, 512], "float32"),
+}
+SEMAPHORES = (["ld%d" % k for k in range(1, NR)] + ["ar%d" % k for k in range(1, NR)]
+              + ["ldo", "sent", "stored", "vs", "acts", "ts", "gs"])
+
+
+def rank_program(g, core, T, topo):
+    rank = T.rank_of(core)
+    if rank is None:
+        return
+    V, A, P, S = g.vector, g.scalar, g.tensor, g.sync
+    sem = T.sem
+    mult, add = AluOpType.mult, AluOpType.add
+
+    def blk(b):
+        return slice(F * b, F * b + F)
+
+    peers = [(rank + k) % NR for k in range(1, NR)]
+
+    for i, b in enumerate(peers):
+        (S, A)[i % 2].dma_start(T.xs[:, blk(b)], T.x[:, blk(b)]).then_inc(sem["ld%d" % (i + 1)], 16)
+    S.dma_start(T.xs[:, blk(rank)], T.x[:, blk(rank)]).then_inc(sem.ldo, 16)
+
+    nv = [0]
+
+    def vwait():
+        if nv[0]:
+            V.wait_ge(sem.vs, nv[0])
+
+    def vdone(ins):
+        ins.then_inc(sem.vs, 1)
+        nv[0] += 1
+        return nv[0]
+
+    k_ones = vdone(V.memset(T.ones[:], 1.0))
+    vwait()
+    vdone(V.memset(T.c128[:], 1.0 / F))
+    vwait()
+    k_eps = vdone(V.memset(T.epsc[:], EPS))
+    vwait()
+    vdone(V.memset(T.rat[:, 0:N1], 4.0))
+    vwait()
+    vdone(V.memset(T.rat[:, N1:N1 + N2], RHO))
+    vwait()
+    vdone(V.tensor_tensor_scan(T.lad[:, 0:N1], T.rat[:, 0:N1], T.ones[:, 0:N1], 2.0 ** -8, mult, mult))
+    vwait()
+    vdone(V.tensor_tensor_scan(T.lad[:, N1:N1 + N2], T.rat[:, N1:N1 + N2], T.ones[:, 0:N2], 2.0 ** -8, mult, mult))
+
+    total = 0
+    for i, b in enumerate(peers):
+        dst = T.cores[b]
+        rid, pid = topo.addr(dst, core)
+        m = topo.mask(core, dst)
+        total += bin(m).count("1")
+        g.wait_ge(sem["ld%d" % (i + 1)], 16)
+        g.remote_dma(out_ap=T.land[:, blk(i)], in_ap=T.xs[:, blk(b)], remote_sem=sem["ar%d" % (i + 1)],
+                     local_sem=sem.sent, pid=pid, routing_id=rid, dma_engine_mask=m)
+    g.wait_ge(sem.vs, k_ones)
+    g.affine_select(T.ident[:], T.ones[:], [[-1, F]], AluOpType.is_equal, 0.0, 0, 1).then_inc(sem.gs, 1)
+
+    P.wait_ge(sem.gs, 1)
+    P.wait_ge(sem.vs, k_eps)
+    P.matmul(T.vps[:, 0:1], T.ident[:], T.epsc[:], start=True, stop=False)
+
+    acc = T.acc[:, 0:F]
+    V.wait_ge(sem.ldo, 16)
+    vwait()
+    vdone(V.tensor_copy(acc, T.xs[:, blk(rank)]))
+    k_s = 0
+    for i in range(NR - 1):
+        src = T.cores[(rank - (i + 1)) % NR]
+        V.wait_ge(sem["ar%d" % (i + 1)], bin(topo.mask(src, core)).count("1"))
+        vwait()
+        k_s = vdone(V.tensor_tensor(acc if i < NR - 2 else T.s[:], acc, T.land[:, blk(i)], add))
+
+    A.wait_ge(sem.vs, k_s)
+    A.activation(T.sq[:], T.s[:], ActivationFunctionType.Square).then_inc(sem.acts, 1)
+    P.wait_ge(sem.acts, 1)
+    P.matmul(T.vps[:, 0:1], T.sq[:], T.c128[:], start=False, stop=True).then_inc(sem.ts, 1)
+
+    v = T.vps[:, 0:1]
+    V.wait_ge(sem.ts, 1)
+    vwait()
+    vdone(V.tensor_scalar(T.fac[:, 0:N1], T.lad[:, 0:N1], v, 0.5, AluOpType.is_gt, AluOpType.max))
+    vwait()
+    k_p1 = vdone(V.tensor_reduce(T.p1[:], T.fac[:, 0:N1], AxisListType.X, mult))
+    vwait()
+    vdone(V.tensor_scalar(T.w[:], v, T.p1[:], T.p1[:], mult, mult))
+    vwait()
+    vdone(V.tensor_scalar(T.fac[:, N1:N1 + N2], T.lad[:, N1:N1 + N2], T.w[:], RHO ** -0.5,
+                          AluOpType.is_gt, AluOpType.max))
+    vwait()
+    vdone(V.tensor_reduce(T.p2[:], T.fac[:, N1:N1 + N2], AxisListType.X, mult))
+    vwait()
+    vdone(V.tensor_scalar(T.t[:], T.w[:], T.p2[:], T.p2[:], mult, mult))
+    vwait()
+    vdone(V.tensor_scalar(T.b[:], T.t[:], 0.375 * KAP ** 5, -1.25 * KAP ** 3, mult, add))
+    vwait()
+    vdone(V.tensor_scalar(T.c[:], T.b[:], T.t[:], 1.875 * KAP, mult, add))
+
+    A.wait_ge(sem.gs, 1)
+    A.wait_ge(sem.vs, k_p1)
+    A.activation(T.d1[:], T.ident[:], ActivationFunctionType.Copy, scale=T.p1[:]).then_inc(sem.acts, 1)
+
+    V.wait_ge(sem.acts, 2)
+    vwait()
+    k_dg = vdone(V.tensor_scalar(T.dg[:], T.d1[:], T.p2[:], T.c[:], mult, mult))
+    P.wait_ge(sem.vs, k_dg)
+    P.matmul(T.rb[:, 0:F], T.ones[:], T.dg[:], start=True, stop=True).then_inc(sem.ts, 1)
+    V.wait_ge(sem.ts, 2)
+    vwait()
+    k_y = vdone(V.tensor_tensor(T.yv[:], T.s[:], T.rb[:, 0:F], mult))
+
+    S.wait_ge(sem.vs, k_y)
+    S.dma_start(T.y[:], T.yv[:]).then_inc(sem.stored, 16)
+    S.wait_ge(sem.stored, 16)
+    g.wait_ge(sem.sent, total)

@@ -3,9 +3,11 @@ from concourse.mybir import AluOpType, AxisListType, ActivationFunctionType
 F = 128
 NR = 5
 EPS = 0.01
-N1, N2 = 67, 63
-RHO = 4.0 ** (1.0 / 64.0)
-KAP = 16.0 * RHO ** -0.25
+N1 = 67
+L2 = 2 * N1
+POLY = [10.11928915, -2.023840715, 0.6071302673, -0.2025897522, 0.07102021267, -0.0248099558, 0.008881186441,
+        -0.004452738974, 0.001854746276, 0.0001541422078, -0.0001316482754, -0.0002536717648, 0.000108066656]
+ND = len(POLY) - 1
 
 SCRATCH = {
     "xs": ("sbuf", [128, NR * F], "float32"),
@@ -14,26 +16,24 @@ SCRATCH = {
     "ident": ("sbuf", [128, F], "float32"),
     "c128": ("sbuf", [128, 1], "float32"),
     "epsc": ("sbuf", [128, 1], "float32"),
-    "rat": ("sbuf", [128, N1 + N2], "float32"),
-    "lad": ("sbuf", [128, N1 + N2], "float32"),
-    "fac": ("sbuf", [128, N1 + N2], "float32"),
+    "rat": ("sbuf", [128, N1], "float32"),
+    "lad": ("sbuf", [128, L2], "float32"),
+    "fac": ("sbuf", [128, L2 + ND], "float32"),
+    "sh": ("sbuf", [128, L2 + ND], "float32"),
+    "sc": ("sbuf", [128, L2 + ND + F - 1], "float32"),
+    "cf": ("sbuf", [128, ND + F - 1], "float32"),
+    "hz": ("sbuf", [128, ND + F - 1], "float32"),
     "p1": ("sbuf", [128, 1], "float32"),
-    "p2": ("sbuf", [128, 1], "float32"),
-    "w": ("sbuf", [128, 1], "float32"),
-    "t": ("sbuf", [128, 1], "float32"),
-    "b": ("sbuf", [128, 1], "float32"),
-    "c": ("sbuf", [128, 1], "float32"),
     "s": ("sbuf", [128, F], "float32"),
     "sq": ("sbuf", [128, F], "float32"),
     "d1": ("sbuf", [128, F], "float32"),
-    "dg": ("sbuf", [128, F], "float32"),
     "yv": ("sbuf", [128, F], "float32"),
     "acc": ("psum", [128, 512], "float32"),
     "vps": ("psum", [128, 512], "float32"),
     "rb": ("psum", [128, 512], "float32"),
 }
 SEMAPHORES = (["ld%d" % k for k in range(1, NR)] + ["ar%d" % k for k in range(1, NR)]
-              + ["ldo", "sent", "stored", "vs", "acts", "ts", "gs"])
+              + ["ldo", "sent", "stored", "ks", "kl", "va", "vb", "vp", "vc", "vd", "ve", "acts", "ts", "gs"])
 
 
 def rank_program(g, core, T, topo):
@@ -53,30 +53,18 @@ def rank_program(g, core, T, topo):
         (S, A)[i % 2].dma_start(T.xs[:, blk(b)], T.x[:, blk(b)]).then_inc(sem["ld%d" % (i + 1)], 16)
     S.dma_start(T.xs[:, blk(rank)], T.x[:, blk(rank)]).then_inc(sem.ldo, 16)
 
-    nv = [0]
-
-    def vwait():
-        if nv[0]:
-            V.wait_ge(sem.vs, nv[0])
-
-    def vdone(ins):
-        ins.then_inc(sem.vs, 1)
-        nv[0] += 1
-        return nv[0]
-
-    k_ones = vdone(V.memset(T.ones[:], 1.0))
-    vwait()
-    vdone(V.memset(T.c128[:], 1.0 / F))
-    vwait()
-    k_eps = vdone(V.memset(T.epsc[:], EPS))
-    vwait()
-    vdone(V.memset(T.rat[:, 0:N1], 4.0))
-    vwait()
-    vdone(V.memset(T.rat[:, N1:N1 + N2], RHO))
-    vwait()
-    vdone(V.tensor_tensor_scan(T.lad[:, 0:N1], T.rat[:, 0:N1], T.ones[:, 0:N1], 2.0 ** -8, mult, mult))
-    vwait()
-    vdone(V.tensor_tensor_scan(T.lad[:, N1:N1 + N2], T.rat[:, N1:N1 + N2], T.ones[:, 0:N2], 2.0 ** -8, mult, mult))
+    fills = [(T.ones[:], 1.0), (T.c128[:], 1.0 / F), (T.epsc[:], EPS), (T.rat[:], 4.0),
+             (T.fac[:, L2:L2 + 1], 256.0), (T.fac[:, L2 + 1:L2 + ND], 1.0),
+             (T.sh[:, 0:L2], 0.0), (T.sh[:, L2:L2 + 1], -2.5), (T.sh[:, L2 + 1:L2 + ND], 0.0),
+             (T.sc[:, L2 + ND:L2 + ND + F - 1], 1.0), (T.cf[:, ND:ND + F - 1], 0.0)]
+    fills += [(T.cf[:, j:j + 1], POLY[ND - 1 - j]) for j in range(ND)]
+    nk = len(fills)
+    for ap, val in fills:
+        V.memset(ap, val).then_inc(sem.ks, 1)
+    V.wait_ge(sem.ks, nk)
+    for h in range(2):
+        V.tensor_tensor_scan(T.lad[:, N1 * h:N1 * h + N1], T.rat[:], T.ones[:, 0:N1], 2.0 ** -8,
+                             mult, mult).then_inc(sem.kl, 1)
 
     total = 0
     for i, b in enumerate(peers):
@@ -87,63 +75,48 @@ def rank_program(g, core, T, topo):
         g.wait_ge(sem["ld%d" % (i + 1)], 16)
         g.remote_dma(out_ap=T.land[:, blk(i)], in_ap=T.xs[:, blk(b)], remote_sem=sem["ar%d" % (i + 1)],
                      local_sem=sem.sent, pid=pid, routing_id=rid, dma_engine_mask=m)
-    g.wait_ge(sem.vs, k_ones)
+    g.wait_ge(sem.ks, nk)
     g.affine_select(T.ident[:], T.ones[:], [[-1, F]], AluOpType.is_equal, 0.0, 0, 1).then_inc(sem.gs, 1)
 
     P.wait_ge(sem.gs, 1)
-    P.wait_ge(sem.vs, k_eps)
+    P.wait_ge(sem.ks, nk)
     P.matmul(T.vps[:, 0:1], T.ident[:], T.epsc[:], start=True, stop=False)
 
     acc = T.acc[:, 0:F]
     V.wait_ge(sem.ldo, 16)
-    vwait()
-    vdone(V.tensor_copy(acc, T.xs[:, blk(rank)]))
-    k_s = 0
+    V.tensor_copy(acc, T.xs[:, blk(rank)]).then_inc(sem.va, 1)
     for i in range(NR - 1):
         src = T.cores[(rank - (i + 1)) % NR]
         V.wait_ge(sem["ar%d" % (i + 1)], bin(topo.mask(src, core)).count("1"))
-        vwait()
-        k_s = vdone(V.tensor_tensor(acc if i < NR - 2 else T.s[:], acc, T.land[:, blk(i)], add))
+        V.wait_ge(sem.va, i + 1)
+        V.tensor_tensor(acc if i < NR - 2 else T.s[:], acc, T.land[:, blk(i)], add).then_inc(sem.va, 1)
 
-    A.wait_ge(sem.vs, k_s)
+    A.wait_ge(sem.va, NR)
     A.activation(T.sq[:], T.s[:], ActivationFunctionType.Square).then_inc(sem.acts, 1)
     P.wait_ge(sem.acts, 1)
     P.matmul(T.vps[:, 0:1], T.sq[:], T.c128[:], start=False, stop=True).then_inc(sem.ts, 1)
 
     v = T.vps[:, 0:1]
+    V.wait_ge(sem.kl, 2)
     V.wait_ge(sem.ts, 1)
-    vwait()
-    vdone(V.tensor_scalar(T.fac[:, 0:N1], T.lad[:, 0:N1], v, 0.5, AluOpType.is_gt, AluOpType.max))
-    vwait()
-    k_p1 = vdone(V.tensor_reduce(T.p1[:], T.fac[:, 0:N1], AxisListType.X, mult))
-    vwait()
-    vdone(V.tensor_scalar(T.w[:], v, T.p1[:], T.p1[:], mult, mult))
-    vwait()
-    vdone(V.tensor_scalar(T.fac[:, N1:N1 + N2], T.lad[:, N1:N1 + N2], T.w[:], RHO ** -0.5,
-                          AluOpType.is_gt, AluOpType.max))
-    vwait()
-    vdone(V.tensor_reduce(T.p2[:], T.fac[:, N1:N1 + N2], AxisListType.X, mult))
-    vwait()
-    vdone(V.tensor_scalar(T.t[:], T.w[:], T.p2[:], T.p2[:], mult, mult))
-    vwait()
-    vdone(V.tensor_scalar(T.b[:], T.t[:], 0.375 * KAP ** 5, -1.25 * KAP ** 3, mult, add))
-    vwait()
-    vdone(V.tensor_scalar(T.c[:], T.b[:], T.t[:], 1.875 * KAP, mult, add))
+    V.tensor_scalar(T.fac[:, 0:L2], T.lad[:], v, 0.5, AluOpType.is_gt, AluOpType.max).then_inc(sem.vb, 1)
+    V.wait_ge(sem.vb, 1)
+    V.tensor_reduce(T.p1[:], T.fac[:, 0:N1], AxisListType.X, mult).then_inc(sem.vp, 1)
+    V.tensor_tensor_scan(T.sc[:, 0:L2 + ND], T.fac[:], T.sh[:], v, mult, add).then_inc(sem.vc, 1)
+    V.wait_ge(sem.vc, 1)
+    V.tensor_tensor_scan(T.hz[:], T.sc[:, L2:L2 + ND + F - 1], T.cf[:], POLY[ND], mult, add).then_inc(sem.vd, 1)
 
     A.wait_ge(sem.gs, 1)
-    A.wait_ge(sem.vs, k_p1)
+    A.wait_ge(sem.vp, 1)
     A.activation(T.d1[:], T.ident[:], ActivationFunctionType.Copy, scale=T.p1[:]).then_inc(sem.acts, 1)
 
-    V.wait_ge(sem.acts, 2)
-    vwait()
-    k_dg = vdone(V.tensor_scalar(T.dg[:], T.d1[:], T.p2[:], T.c[:], mult, mult))
-    P.wait_ge(sem.vs, k_dg)
-    P.matmul(T.rb[:, 0:F], T.ones[:], T.dg[:], start=True, stop=True).then_inc(sem.ts, 1)
+    P.wait_ge(sem.vd, 1)
+    P.wait_ge(sem.acts, 2)
+    P.matmul(T.rb[:, 0:F], T.hz[:, ND - 1:ND - 1 + F], T.d1[:], start=True, stop=True).then_inc(sem.ts, 1)
     V.wait_ge(sem.ts, 2)
-    vwait()
-    k_y = vdone(V.tensor_tensor(T.yv[:], T.s[:], T.rb[:, 0:F], mult))
+    V.tensor_tensor(T.yv[:], T.s[:], T.rb[:, 0:F], mult).then_inc(sem.ve, 1)
 
-    S.wait_ge(sem.vs, k_y)
+    S.wait_ge(sem.ve, 1)
     S.dma_start(T.y[:], T.yv[:]).then_inc(sem.stored, 16)
     S.wait_ge(sem.stored, 16)
     g.wait_ge(sem.sent, total)

from concourse.mybir import AluOpType, AxisListType, ActivationFunctionType

F = 128
NR = 5
EPS = 0.01
N1 = 67
L2 = 2 * N1
POLY = [10.11928915, -2.023840715, 0.6071302673, -0.2025897522, 0.07102021267, -0.0248099558, 0.008881186441,
        -0.004452738974, 0.001854746276, 0.0001541422078, -0.0001316482754, -0.0002536717648, 0.000108066656]
ND = len(POLY) - 1

SCRATCH = {
    "xs": ("sbuf", [128, NR * F], "float32"),
    "land": ("sbuf", [128, (NR - 1) * F], "float32"),
    "ones": ("sbuf", [128, F], "float32"),
    "ident": ("sbuf", [128, F], "float32"),
    "c128": ("sbuf", [128, 1], "float32"),
    "epsc": ("sbuf", [128, 1], "float32"),
    "rat": ("sbuf", [128, N1], "float32"),
    "lad": ("sbuf", [128, L2], "float32"),
    "fac": ("sbuf", [128, L2 + ND], "float32"),
    "sh": ("sbuf", [128, L2 + ND], "float32"),
    "sc": ("sbuf", [128, L2 + ND + F - 1], "float32"),
    "cf": ("sbuf", [128, ND + F - 1], "float32"),
    "hz": ("sbuf", [128, ND + F - 1], "float32"),
    "p1": ("sbuf", [128, 1], "float32"),
    "s": ("sbuf", [128, F], "float32"),
    "sq": ("sbuf", [128, F], "float32"),
    "d1": ("sbuf", [128, F], "float32"),
    "yv": ("sbuf", [128, F], "float32"),
    "acc": ("psum", [128, 512], "float32"),
    "vps": ("psum", [128, 512], "float32"),
    "rb": ("psum", [128, 512], "float32"),
}
SEMAPHORES = (["ld%d" % k for k in range(1, NR)] + ["ar%d" % k for k in range(1, NR)]
              + ["ldo", "sent", "stored", "ks", "kl", "va", "vb", "vp", "vc", "vd", "ve", "acts", "ts", "gs"])


def rank_program(g, core, T, topo):
    rank = T.rank_of(core)
    if rank is None:
        return
    V, A, P, S = g.vector, g.scalar, g.tensor, g.sync
    sem = T.sem
    mult, add = AluOpType.mult, AluOpType.add

    def blk(b):
        return slice(F * b, F * b + F)

    peers = [(rank + k) % NR for k in range(1, NR)]

    for i, b in enumerate(peers):
        (S, A)[i % 2].dma_start(T.xs[:, blk(b)], T.x[:, blk(b)]).then_inc(sem["ld%d" % (i + 1)], 16)
    S.dma_start(T.xs[:, blk(rank)], T.x[:, blk(rank)]).then_inc(sem.ldo, 16)

    fills = [(T.ones[:], 1.0), (T.c128[:], 1.0 / F), (T.epsc[:], EPS), (T.rat[:], 4.0),
             (T.fac[:, L2:L2 + 1], 256.0), (T.fac[:, L2 + 1:L2 + ND], 1.0),
             (T.sh[:, 0:L2], 0.0), (T.sh[:, L2:L2 + 1], -2.5), (T.sh[:, L2 + 1:L2 + ND], 0.0),
             (T.sc[:, L2 + ND:L2 + ND + F - 1], 1.0), (T.cf[:, ND:ND + F - 1], 0.0)]
    fills += [(T.cf[:, j:j + 1], POLY[ND - 1 - j]) for j in range(ND)]
    nk = len(fills)
    for ap, val in fills:
        V.memset(ap, val).then_inc(sem.ks, 1)
    V.wait_ge(sem.ks, nk)
    for h in range(2):
        V.tensor_tensor_scan(T.lad[:, N1 * h:N1 * h + N1], T.rat[:], T.ones[:, 0:N1], 2.0 ** -8,
                             mult, mult).then_inc(sem.kl, 1)

    total = 0
    for i, b in enumerate(peers):
        dst = T.cores[b]
        rid, pid = topo.addr(dst, core)
        m = topo.mask(core, dst)
        total += bin(m).count("1")
        g.wait_ge(sem["ld%d" % (i + 1)], 16)
        g.remote_dma(out_ap=T.land[:, blk(i)], in_ap=T.xs[:, blk(b)], remote_sem=sem["ar%d" % (i + 1)],
                     local_sem=sem.sent, pid=pid, routing_id=rid, dma_engine_mask=m)
    g.wait_ge(sem.ks, nk)
    g.affine_select(T.ident[:], T.ones[:], [[-1, F]], AluOpType.is_equal, 0.0, 0, 1).then_inc(sem.gs, 1)

    P.wait_ge(sem.gs, 1)
    P.wait_ge(sem.ks, nk)
    P.matmul(T.vps[:, 0:1], T.ident[:], T.epsc[:], start=True, stop=False)

    acc = T.acc[:, 0:F]
    V.wait_ge(sem.ldo, 16)
    V.tensor_copy(acc, T.xs[:, blk(rank)]).then_inc(sem.va, 1)
    for i in range(NR - 1):
        src = T.cores[(rank - (i + 1)) % NR]
        V.wait_ge(sem["ar%d" % (i + 1)], bin(topo.mask(src, core)).count("1"))
        V.wait_ge(sem.va, i + 1)
        V.tensor_tensor(acc if i < NR - 2 else T.s[:], acc, T.land[:, blk(i)], add).then_inc(sem.va, 1)

    A.wait_ge(sem.va, NR)
    A.activation(T.sq[:], T.s[:], ActivationFunctionType.Square).then_inc(sem.acts, 1)
    P.wait_ge(sem.acts, 1)
    P.matmul(T.vps[:, 0:1], T.sq[:], T.c128[:], start=False, stop=True).then_inc(sem.ts, 1)

    v = T.vps[:, 0:1]
    V.wait_ge(sem.kl, 2)
    V.wait_ge(sem.ts, 1)
    V.tensor_scalar(T.fac[:, 0:L2], T.lad[:], v, 0.5, AluOpType.is_gt, AluOpType.max).then_inc(sem.vb, 1)
    V.wait_ge(sem.vb, 1)
    V.tensor_reduce(T.p1[:], T.fac[:, 0:N1], AxisListType.X, mult).then_inc(sem.vp, 1)
    V.tensor_tensor_scan(T.sc[:, 0:L2 + ND], T.fac[:], T.sh[:], v, mult, add).then_inc(sem.vc, 1)
    V.wait_ge(sem.vc, 1)
    V.tensor_tensor_scan(T.hz[:], T.sc[:, L2:L2 + ND + F - 1], T.cf[:], POLY[ND], mult, add).then_inc(sem.vd, 1)

    A.wait_ge(sem.gs, 1)
    A.wait_ge(sem.vp, 1)
    A.activation(T.d1[:], T.ident[:], ActivationFunctionType.Copy, scale=T.p1[:]).then_inc(sem.acts, 1)

    P.wait_ge(sem.vd, 1)
    P.wait_ge(sem.acts, 2)
    P.matmul(T.rb[:, 0:F], T.hz[:, ND - 1:ND - 1 + F], T.d1[:], start=True, stop=True).then_inc(sem.ts, 1)
    V.wait_ge(sem.ts, 2)
    V.tensor_tensor(T.yv[:], T.s[:], T.rb[:, 0:F], mult).then_inc(sem.ve, 1)

    S.wait_ge(sem.ve, 1)
    S.dma_start(T.y[:], T.yv[:]).then_inc(sem.stored, 16)
    S.wait_ge(sem.stored, 16)
    g.wait_ge(sem.sent, total)
